import numpy as np
import ml_dtypes


def mxq(x, axis, fmt="e4m3"):
    dtype, down = {"e4m3": (ml_dtypes.float8_e4m3fn, 7), "e5m2": (ml_dtypes.float8_e5m2, 14)}[fmt]
    v = np.moveaxis(np.asarray(x, np.float32).astype(ml_dtypes.bfloat16).astype(np.float64), axis, -1)
    blocks = v.reshape(v.shape[:-1] + (-1, 32))
    amax = np.abs(blocks).max(-1, keepdims=True)
    byte = np.maximum(np.where(amax > 0, np.frexp(amax)[1] - 1 + 127, 0) - down, 1)
    scale = np.exp2(byte - 127.0)
    codes = (blocks / scale).astype(np.float32).astype(dtype).astype(np.float64)
    return np.moveaxis((codes * scale).reshape(v.shape), -1, axis)


WIDE = False


def mx_kscale(k):
    if not WIDE:
        return np.ones(k)
    levels = np.array([24, -24, 12, -12, 0])
    if k % 512:
        return np.exp2(np.random.permutation(np.resize(levels, k // 32))).repeat(32)
    a = np.empty((k // 512, 16))
    for p in range(k // 512):
        a[p, :8] = np.random.permutation(np.resize(levels, 8))
        for g in range(8):
            far = levels[np.abs(levels - a[p, g]) >= 10]
            a[p, g + 8] = far[np.random.randint(len(far))]
    return np.exp2(a.ravel()).repeat(32)


def f64(x):
    return np.asarray(x).astype(np.float64)


def striped8(idx):
    return np.concatenate([v.reshape(-1, 16).T for v in idx]).astype(np.uint16)


def unstriped8(offs):
    return np.stack([offs[16 * g:16 * g + 16].T.reshape(-1) for g in range(8)]).astype(np.int64)


E2M1 = np.array([0.0, 0.5, 1.0, 1.5, 2.0, 3.0, 4.0, 6.0, -0.0, -0.5, -1.0, -1.5, -2.0, -3.0, -4.0, -6.0])


def pack_weight(w, fmt):
    k, n = w.shape
    w = f64(np.asarray(w, np.float32).astype(ml_dtypes.bfloat16)).reshape(k // 32, 32, n)
    amax = np.abs(w).max(1)
    if fmt == "e4m3":
        byte = np.frexp(amax)[1] - 1 + 127 - 7
    else:
        mant, ex = np.frexp(amax / 6.0)
        byte = np.where(mant > 0.5, ex, ex - 1) + 127
    byte = np.clip(np.where(amax > 0, byte, 1), 1, 254)
    scaled = (w * np.exp2(127.0 - byte)[:, None, :]).reshape(k, n).astype(np.float32)
    by_word = np.ascontiguousarray(scaled.reshape(k // 512, 128, 4, n).transpose(0, 1, 3, 2))
    if fmt == "e4m3":
        words = by_word.astype(ml_dtypes.float8_e4m3fn).view(np.uint8)
    else:
        c = by_word.astype(ml_dtypes.float4_e2m1fn).view(np.uint8) & 0xF
        words = (c[..., 0::2] | (c[..., 1::2] << 4)).reshape(k // 512, 128, 2 * n)
    return np.ascontiguousarray(words), np.ascontiguousarray(byte.astype(np.uint8).reshape(k // 512, 16, n))


def unpack_weight(words, scales, fmt):
    g, _, n = scales.shape
    words = np.ascontiguousarray(words).reshape(g, 128, n, -1)
    if fmt == "e4m3":
        vals = words.view(ml_dtypes.float8_e4m3fn).astype(np.float64)
    else:
        nib = np.empty((g, 128, n, 4), np.uint8)
        nib[..., 0::2] = words & 0xF
        nib[..., 1::2] = words >> 4
        vals = E2M1[nib]
    vals = vals * np.repeat(np.exp2(scales.astype(np.float64) - 127.0), 8, axis=1)[..., None]
    return vals.transpose(0, 1, 3, 2).reshape(g * 512, n)


def silu(f):
    return f / (1.0 + np.exp(-np.maximum(f, -700.0)))


K, N, T, J = 512, 512, 2048, 512


def setup_inputs():
    n = np.random.standard_normal
    s = mx_kscale(K)[:, None]
    p_w = pack_weight(n((K, N)) / np.sqrt(K) / s, "e2m1")
    return {
        "xT": (n((K, T)) * s).astype(np.float32),
        "wgt": np.repeat(np.random.uniform(0.5, 2.0, (8, 2 * J)), 16, axis=0).astype(np.float32),
        "w_words": p_w[0],
        "w_scales": p_w[1],
        "iw0": (np.random.uniform(0.1, 0.9, (N, J))).astype(np.float32),
        "iw1": (np.random.uniform(0.1, 0.9, (N, J))).astype(np.float32),
        "b": (0.3 * n(N)).astype(np.float32),
        "offs": striped8(np.stack([np.concatenate([np.random.permutation(T)[:J] for _ in range(2)]) for _ in range(8)])),
    }


def reference(xT, wgt, w_words, w_scales, iw0, iw1, b, offs):
    idx = unstriped8(offs)
    rows = np.arange(K)
    xg = f64(wgt)[rows // 4 % 128] * f64(xT)[rows[:, None], idx[rows % 512 // 64]]
    xT_ = mxq(xg, 0, "e4m3").reshape(K, 2, J)
    w_ = unpack_weight(w_words, w_scales, "e2m1")
    a0 = w_.T @ xT_[:, 0]
    a1 = w_.T @ xT_[:, 1]
    return silu(a0 * f64(iw0) + a1 * f64(iw1) + f64(b)[:, None])

@@ -1,0 +1,146 @@
+from contextlib import ExitStack
+
+import concourse.mybir as mybir
+
+K, N, T, J = 512, 512, 2048, 512
+FLOPS = 2 * K * N * 2 * J
+
+F32 = mybir.dt.float32
+BF16 = mybir.dt.bfloat16
+I32 = mybir.dt.int32
+U32 = mybir.dt.uint32
+U16 = mybir.dt.uint16
+U8 = mybir.dt.uint8
+FP8X4 = mybir.dt.float8_e4m3fn_x4
+FP4X4 = mybir.dt.float4_e2m1fn_x4
+MULT = mybir.AluOpType.mult
+ADD = mybir.AluOpType.add
+SILU = mybir.ActivationFunctionType.Silu
+
+P = 128
+PACK = 4
+PICKS = 2
+NT = N // P
+BANK = 512
+SLICES = ((0, 128), (128, 128), (256, 256))
+HALF = J // 2
+
+
+def tile_list_soft_silu_kernel(tc, xT, wgt, w_words, w_scales, iw0, iw1, b, offs, out):
+    nc = tc.nc
+    with ExitStack() as ctx:
+        keep = ctx.enter_context(tc.tile_pool(name="keep", bufs=1))
+        psum = ctx.enter_context(tc.psum_pool(name="psum", bufs=1))
+
+        offsets = keep.tile([P, PICKS * J // 16], U16, name="offsets")
+        nc.sync.dma_start(offsets[:], offs)
+
+        x_rows = xT.rearrange("(p i) t -> i p t", i=PACK)
+        planes = [keep.tile([P, T], F32, name=f"plane{i}") for i in range(PACK)]
+        head_w = [keep.tile([P, J], F32, name=f"head_w{c}") for c in range(PICKS)]
+        nc.sync.dma_start(head_w[0][:], wgt[:, 0:J])
+        nc.sync.dma_start(planes[0][:], x_rows[0])
+        nc.sync.dma_start(head_w[1][:], wgt[:, J : 2 * J])
+        for i in range(1, PACK):
+            nc.sync.dma_start(planes[i][:], x_rows[i])
+
+        w_codes = keep.tile([P, 2 * N], U8, name="w_codes", align_bytes=64)
+        nc.sync.dma_start(w_codes[:].bitcast(I32), w_words[0].bitcast(I32))
+
+        pool_w = [keep.tile([P, PICKS, NT, HALF], F32, name=f"pool_w{h}") for h in range(2)]
+        for h in range(2):
+            for c, iw in enumerate((iw0, iw1)):
+                nc.sync.dma_start(pool_w[h][:, c], iw[:, h * HALF : (h + 1) * HALF].rearrange("(t p) j -> p t j", p=P))
+
+        bias = keep.tile([P, NT], F32, name="bias")
+        with nc.allow_non_contiguous_dma(reason="one bias value a partition"):
+            nc.sync.dma_start(bias[:], b.rearrange("(t p) -> p t", p=P))
+
+        w_plane = keep.tile([P, N], U8, name="w_plane", align_bytes=64)
+        nc.gpsimd.memset(w_plane[:].bitcast(I32), 0)
+        for q in range(4):
+            nc.gpsimd.dma_start(w_plane[32 * q : 32 * q + 4, :].bitcast(I32), w_scales[0, 4 * q : 4 * q + 4, :].bitcast(I32))
+
+        warm_in = keep.tile([P, 1], F32, name="warm_in")
+        warm_out = keep.tile([P, 1], F32, name="warm_out")
+        nc.vector.memset(warm_in[:], 0.0)
+        nc.scalar.activation(warm_out[:], warm_in[:], SILU)
+
+        picked = keep.tile([P, PACK, PICKS, J], F32, name="picked")
+
+        def gather(i, c, j0, j1):
+            first = (c * J + j0) // 16
+            last = (c * J + j1) // 16
+            nc.vector.tensor_tensor(picked[:, i, c, j0:j1], planes[i][:].indirect(offsets[:, first:last]), head_w[c][:, j0:j1], MULT)
+
+        for i in range(PACK - 1):
+            for c in range(PICKS):
+                gather(i, c, 0, J)
+        for j0, w in SLICES:
+            for c in range(PICKS):
+                gather(PACK - 1, c, j0, j0 + w)
+
+        def weave(copy, woven, j0, w, picks):
+            copy(
+                woven[:, picks].rearrange("p c (g e) i -> p c g i e", e=4),
+                picked[:, :, picks, j0 : j0 + w].rearrange("p i c (g e) -> p c g i e", e=4),
+            )
+
+        banks = []
+        for s, (j0, w) in enumerate(SLICES):
+            woven = keep.tile([P, PICKS, w, PACK], BF16, name=f"woven{s}", tag=f"stage{s}", align_bytes=64)
+            if s < len(SLICES) - 1 or not True:
+                weave(nc.scalar.copy, woven, j0, w, slice(0, PICKS))
+            else:
+                weave(nc.scalar.copy, woven, j0, w, slice(0, 1))
+                weave(nc.vector.tensor_copy, woven, j0, w, slice(1, 2))
+            codes = keep.tile([P, PICKS * w], U32, name=f"codes{s}", align_bytes=64)
+            scales = keep.tile([P, PICKS * w], U8, name=f"scales{s}", align_bytes=64)
+            nc.vector.quantize_mx(codes[:].bitcast(FP8X4), scales[:], woven[:].rearrange("p c w i -> p (c w i)"))
+            per_bank = BANK // (PICKS * w)
+            for u in range(NT // per_bank):
+                bank = psum.tile([P, per_bank, PICKS, w], F32, name=f"bank{s}_{u}")
+                banks.append(bank)
+                for v in range(per_bank):
+                    t = per_bank * u + v
+                    nc.tensor.matmul_mx(
+                        bank[:, v].rearrange("p c j -> p (c j)"),
+                        lhsT=w_codes[:, 2 * P * t : 2 * P * (t + 1)].bitcast(FP4X4),
+                        lhsT_scale=w_plane[:, P * t : P * (t + 1)],
+                        rhs=codes[:].bitcast(FP8X4),
+                        rhs_scale=scales[:],
+                        start=True,
+                        stop=True,
+                    )
+
+        out_rows = out.rearrange("(t p) j -> p t j", p=P)
+        terms = []
+        for s, (j0, w) in enumerate(SLICES):
+            h, jh = divmod(j0, HALF)
+            per_bank = BANK // (PICKS * w)
+            term = keep.tile([P, PICKS, NT, w], F32, name=f"terms{s}")
+            terms.append(term)
+            for u in range(NT // per_bank):
+                rows = slice(per_bank * u, per_bank * (u + 1))
+                nc.vector.tensor_tensor(
+                    term[:, :, rows, :].rearrange("p c t j -> p t c j"),
+                    banks.pop(0)[:],
+                    pool_w[h][:, :, rows, jh : jh + w].rearrange("p c t j -> p t c j"),
+                    MULT,
+                )
+
+        def finish(name, engine, s, rows, tag):
+            j0, w = SLICES[s]
+            count = rows.stop - rows.start
+            summed = keep.tile([P, count, w], F32, name=f"summed{name}", tag=tag, align_bytes=64)
+            result = keep.tile([P, count, w], F32, name=f"result{name}")
+            engine.tensor_tensor(summed[:], terms[s][:, 0, rows, :], terms[s][:, 1, rows, :], ADD)
+            for t in range(count):
+                nt = rows.start + t
+                nc.scalar.activation(result[:, t, :], summed[:, t, :], SILU, bias=bias[:, nt : nt + 1])
+            nc.sync.dma_start(out_rows[:, rows, j0 : j0 + w], result[:])
+
+        finish("a", nc.gpsimd, 0, slice(0, NT), "stage2")
+        finish("b", nc.gpsimd, 1, slice(0, NT), "stage1")
+        for t in range(NT):
+            finish(f"c{t}", nc.gpsimd if t < 1 else nc.vector, 2, slice(t, t + 1), f"last{t}")

@@ -22,6 +22,9 @@ PACK = 4
 PICKS = 2
 NT = N // P
 BANK = 512
+RUN = 64
+DEAL_STEP = PICKS * J - RUN
+DEAL_START = 7 * PICKS * J + J - RUN
 SLICES = ((0, 128), (128, 128), (256, 256))
 HALF = J // 2
 
@@ -32,20 +35,35 @@ def tile_list_soft_silu_kernel(tc, xT, wgt, w_words, w_scales, iw0, iw1, b, offs
         keep = ctx.enter_context(tc.tile_pool(name="keep", bufs=1))
         psum = ctx.enter_context(tc.psum_pool(name="psum", bufs=1))
 
-        offsets = keep.tile([P, PICKS * J // 16], U16, name="offsets")
-        nc.sync.dma_start(offsets[:], offs)
-
         x_rows = xT.rearrange("(p i) t -> i p t", i=PACK)
         planes = [keep.tile([P, T], F32, name=f"plane{i}") for i in range(PACK)]
-        head_w = [keep.tile([P, J], F32, name=f"head_w{c}") for c in range(PICKS)]
-        nc.sync.dma_start(head_w[0][:], wgt[:, 0:J])
+        head_w = keep.tile([P, PICKS, J], F32, name="head_w", align_bytes=64)
+        offsets = keep.tile([P, PICKS * J // 16], U16, name="offsets")
+        dealt = keep.tile([P, PICKS, RUN], F32, name="dealt", align_bytes=64)
+        flat = wgt.rearrange("r c -> (r c)")[DEAL_START : DEAL_START + P * DEAL_STEP].rearrange("(p s) -> p s", s=DEAL_STEP)
+        nc.sync.dma_start(dealt[:], flat[:, 0 : J + RUN].rearrange("p (c j) -> p c j", j=RUN)[:, 0 : J // RUN + 1 : J // RUN, :])
         nc.sync.dma_start(planes[0][:], x_rows[0])
-        nc.sync.dma_start(head_w[1][:], wgt[:, J : 2 * J])
+        nc.sync.dma_start(offsets[:], offs)
         for i in range(1, PACK):
             nc.sync.dma_start(planes[i][:], x_rows[i])
 
+        turned = keep.tile([P, PICKS, 2, 2, 16], F32, name="turned", align_bytes=64)
+        nc.vector.transpose(turned[:].rearrange("p c u e a -> p (c u e a)"), dealt[:].rearrange("p c j -> p (c j)"))
+        for c in range(PICKS):
+            spread = keep.tile([P, J], F32, name=f"spread{c}", align_bytes=64)
+            nc.vector.tensor_copy(
+                spread[:].rearrange("p (m u e r) -> p m u e r", u=2, e=2, r=16),
+                turned[:, c].rearrange("p u e (a o) -> p a u e o", o=1)[:, 0:8][:, ::-1].to_broadcast([P, 8, 2, 2, 16]),
+            )
+            nc.vector.transpose(head_w[:, c], spread[:])
+
         w_codes = keep.tile([P, 2 * N], U8, name="w_codes", align_bytes=64)
         nc.sync.dma_start(w_codes[:].bitcast(I32), w_words[0].bitcast(I32))
+
+        w_plane = keep.tile([P, N], U8, name="w_plane", align_bytes=64)
+        nc.gpsimd.memset(w_plane[:].bitcast(I32), 0)
+        for q in range(4):
+            nc.sync.dma_start(w_plane[32 * q : 32 * q + 4, :].bitcast(I32), w_scales[0, 4 * q : 4 * q + 4, :].bitcast(I32))
 
         pool_w = [keep.tile([P, PICKS, NT, HALF], F32, name=f"pool_w{h}") for h in range(2)]
         for h in range(2):
@@ -56,26 +74,20 @@ def tile_list_soft_silu_kernel(tc, xT, wgt, w_words, w_scales, iw0, iw1, b, offs
         with nc.allow_non_contiguous_dma(reason="one bias value a partition"):
             nc.sync.dma_start(bias[:], b.rearrange("(t p) -> p t", p=P))
 
-        w_plane = keep.tile([P, N], U8, name="w_plane", align_bytes=64)
-        nc.gpsimd.memset(w_plane[:].bitcast(I32), 0)
-        for q in range(4):
-            nc.gpsimd.dma_start(w_plane[32 * q : 32 * q + 4, :].bitcast(I32), w_scales[0, 4 * q : 4 * q + 4, :].bitcast(I32))
-
-        warm_in = keep.tile([P, 1], F32, name="warm_in")
-        warm_out = keep.tile([P, 1], F32, name="warm_out")
-        nc.vector.memset(warm_in[:], 0.0)
-        nc.scalar.activation(warm_out[:], warm_in[:], SILU)
-
         picked = keep.tile([P, PACK, PICKS, J], F32, name="picked")
 
         def gather(i, c, j0, j1):
             first = (c * J + j0) // 16
             last = (c * J + j1) // 16
-            nc.vector.tensor_tensor(picked[:, i, c, j0:j1], planes[i][:].indirect(offsets[:, first:last]), head_w[c][:, j0:j1], MULT)
+            nc.vector.tensor_tensor(picked[:, i, c, j0:j1], planes[i][:].indirect(offsets[:, first:last]), head_w[:, c, j0:j1], MULT)
 
         for i in range(PACK - 1):
-            for c in range(PICKS):
-                gather(i, c, 0, J)
+            nc.vector.tensor_tensor(
+                picked[:, i].rearrange("p c j -> p (c j)"),
+                planes[i][:].indirect(offsets[:]),
+                head_w[:].rearrange("p c j -> p (c j)"),
+                MULT,
+            )
         for j0, w in SLICES:
             for c in range(PICKS):
                 gather(PACK - 1, c, j0, j0 + w)
@@ -138,7 +150,7 @@ def tile_list_soft_silu_kernel(tc, xT, wgt, w_words, w_scales, iw0, iw1, b, offs
             for t in range(count):
                 nt = rows.start + t
                 nc.scalar.activation(result[:, t, :], summed[:, t, :], SILU, bias=bias[:, nt : nt + 1])
-            nc.sync.dma_start(out_rows[:, rows, j0 : j0 + w], result[:])
+            (nc.scalar if name == "c3" else nc.sync).dma_start(out_rows[:, rows, j0 : j0 + w], result[:])
 
         finish("a", nc.gpsimd, 0, slice(0, NT), "stage2")
         finish("b", nc.gpsimd, 1, slice(0, NT), "stage1")

@@ -37,14 +37,17 @@ def tile_list_soft_silu_kernel(tc, xT, wgt, w_words, w_scales, iw0, iw1, b, offs
 
         x_rows = xT.rearrange("(p i) t -> i p t", i=PACK)
         planes = [keep.tile([P, T], F32, name=f"plane{i}") for i in range(PACK)]
-        head_w = keep.tile([P, PICKS, J], F32, name="head_w", align_bytes=64)
+        work = keep.tile([P, (PACK + 1) * PICKS, J], F32, name="work", align_bytes=64)
+        picked = work[:, 0 : PACK * PICKS, :].rearrange("p (i c) j -> p i c j", c=PICKS)
+        head_start = PACK * PICKS * J - HALF
+        head_w = work[:].rearrange("p r j -> p (r j)")[:, head_start : head_start + PICKS * J].rearrange("p (c j) -> p c j", c=PICKS)
         offsets = keep.tile([P, PICKS * J // 16], U16, name="offsets")
         dealt = keep.tile([P, PICKS, RUN], F32, name="dealt", align_bytes=64)
         flat = wgt.rearrange("r c -> (r c)")[DEAL_START : DEAL_START + P * DEAL_STEP].rearrange("(p s) -> p s", s=DEAL_STEP)
         nc.sync.dma_start(dealt[:], flat[:, 0 : J + RUN].rearrange("p (c j) -> p c j", j=RUN)[:, 0 : J // RUN + 1 : J // RUN, :])
         nc.sync.dma_start(planes[0][:], x_rows[0])
         nc.sync.dma_start(offsets[:], offs)
-        for i in range(1, PACK):
+        for i in (1, 3, 2):
             nc.sync.dma_start(planes[i][:], x_rows[i])
 
         turned = keep.tile([P, PICKS, 2, 2, 16], F32, name="turned", align_bytes=64)
@@ -74,41 +77,37 @@ def tile_list_soft_silu_kernel(tc, xT, wgt, w_words, w_scales, iw0, iw1, b, offs
         with nc.allow_non_contiguous_dma(reason="one bias value a partition"):
             nc.sync.dma_start(bias[:], b.rearrange("(t p) -> p t", p=P))
 
-        picked = keep.tile([P, PACK, PICKS, J], F32, name="picked")
 
         def gather(i, c, j0, j1):
             first = (c * J + j0) // 16
             last = (c * J + j1) // 16
             nc.vector.tensor_tensor(picked[:, i, c, j0:j1], planes[i][:].indirect(offsets[:, first:last]), head_w[:, c, j0:j1], MULT)
 
-        for i in range(PACK - 1):
+        for i in (0, 1):
             nc.vector.tensor_tensor(
                 picked[:, i].rearrange("p c j -> p (c j)"),
                 planes[i][:].indirect(offsets[:]),
-                head_w[:].rearrange("p c j -> p (c j)"),
+                head_w.rearrange("p c j -> p (c j)"),
                 MULT,
             )
-        for j0, w in SLICES:
-            for c in range(PICKS):
-                gather(PACK - 1, c, j0, j0 + w)
+        held = PICKS * J - HALF
+        nc.vector.tensor_tensor(
+            picked[:, 3].rearrange("p c j -> p (c j)")[:, 0:held],
+            planes[3][:].indirect(offsets[:, 0 : held // 16]),
+            head_w.rearrange("p c j -> p (c j)")[:, 0:held],
+            MULT,
+        )
 
-        def weave(copy, woven, j0, w, picks):
-            copy(
-                woven[:, picks].rearrange("p c (g e) i -> p c g i e", e=4),
+        def quantise(woven, codes, scales, j0, w, picks):
+            nc.scalar.copy(
+                woven.rearrange("p c (g e) i -> p c g i e", e=4),
                 picked[:, :, picks, j0 : j0 + w].rearrange("p i c (g e) -> p c g i e", e=4),
             )
+            nc.vector.quantize_mx(codes.bitcast(FP8X4), scales, woven.rearrange("p c w i -> p (c w i)"))
 
         banks = []
-        for s, (j0, w) in enumerate(SLICES):
-            woven = keep.tile([P, PICKS, w, PACK], BF16, name=f"woven{s}", tag=f"stage{s}", align_bytes=64)
-            if s < len(SLICES) - 1 or not True:
-                weave(nc.scalar.copy, woven, j0, w, slice(0, PICKS))
-            else:
-                weave(nc.scalar.copy, woven, j0, w, slice(0, 1))
-                weave(nc.vector.tensor_copy, woven, j0, w, slice(1, 2))
-            codes = keep.tile([P, PICKS * w], U32, name=f"codes{s}", align_bytes=64)
-            scales = keep.tile([P, PICKS * w], U8, name=f"scales{s}", align_bytes=64)
-            nc.vector.quantize_mx(codes[:].bitcast(FP8X4), scales[:], woven[:].rearrange("p c w i -> p (c w i)"))
+
+        def project(s, codes, scales, w):
             per_bank = BANK // (PICKS * w)
             for u in range(NT // per_bank):
                 bank = psum.tile([P, per_bank, PICKS, w], F32, name=f"bank{s}_{u}")
@@ -125,34 +124,64 @@ def tile_list_soft_silu_kernel(tc, xT, wgt, w_words, w_scales, iw0, iw1, b, offs
                         stop=True,
                     )
 
-        out_rows = out.rearrange("(t p) j -> p t j", p=P)
-        terms = []
-        for s, (j0, w) in enumerate(SLICES):
+        codes = [keep.tile([P, PICKS * w], U32, name=f"codes{s}", align_bytes=64) for s, (j0, w) in enumerate(SLICES)]
+        scales = [keep.tile([P, PICKS * w], U8, name=f"scales{s}", align_bytes=64) for s, (j0, w) in enumerate(SLICES)]
+        terms = [keep.tile([P, PICKS, NT, w], F32, name=f"terms{s}") for s, (j0, w) in enumerate(SLICES)]
+        stages = [keep.tile([P, BANK], F32, name=f"stage{n}", align_bytes=64) for n in range(4)]
+
+        def both_picks(s):
+            j0, w = SLICES[s]
+            woven = stages[s][:].bitcast(BF16).rearrange("p (c w i) -> p c w i", c=PICKS, i=PACK)
+            quantise(woven, codes[s][:], scales[s][:], j0, w, slice(0, PICKS))
+            project(s, codes[s], scales[s], w)
+
+        def one_pick(s, c):
+            j0, w = SLICES[s]
+            woven = stages[s + c][:].bitcast(BF16).rearrange("p (c w i) -> p c w i", c=1, i=PACK)
+            quantise(woven, codes[s][:, c * w : (c + 1) * w], scales[s][:, c * w : (c + 1) * w], j0, w, slice(c, c + 1))
+
+        def weigh(s, u):
+            j0, w = SLICES[s]
             h, jh = divmod(j0, HALF)
             per_bank = BANK // (PICKS * w)
-            term = keep.tile([P, PICKS, NT, w], F32, name=f"terms{s}")
-            terms.append(term)
-            for u in range(NT // per_bank):
-                rows = slice(per_bank * u, per_bank * (u + 1))
-                nc.vector.tensor_tensor(
-                    term[:, :, rows, :].rearrange("p c t j -> p t c j"),
-                    banks.pop(0)[:],
-                    pool_w[h][:, :, rows, jh : jh + w].rearrange("p c t j -> p t c j"),
-                    MULT,
-                )
+            rows = slice(per_bank * u, per_bank * (u + 1))
+            nc.vector.tensor_tensor(
+                terms[s][:, :, rows, :].rearrange("p c t j -> p t c j"),
+                banks.pop(0)[:],
+                pool_w[h][:, :, rows, jh : jh + w].rearrange("p c t j -> p t c j"),
+                MULT,
+            )
 
-        def finish(name, engine, s, rows, tag):
+        out_rows = out.rearrange("(t p) j -> p t j", p=P)
+
+        def finish(engine, queue, s, t0, count, summed):
             j0, w = SLICES[s]
-            count = rows.stop - rows.start
-            summed = keep.tile([P, count, w], F32, name=f"summed{name}", tag=tag, align_bytes=64)
-            result = keep.tile([P, count, w], F32, name=f"result{name}")
-            engine.tensor_tensor(summed[:], terms[s][:, 0, rows, :], terms[s][:, 1, rows, :], ADD)
+            result = keep.tile([P, count, w], F32, name=f"result{s}_{t0}")
+            engine.tensor_tensor(summed, terms[s][:, 0, t0 : t0 + count, :], terms[s][:, 1, t0 : t0 + count, :], ADD)
             for t in range(count):
-                nt = rows.start + t
-                nc.scalar.activation(result[:, t, :], summed[:, t, :], SILU, bias=bias[:, nt : nt + 1])
-            (nc.scalar if name == "c3" else nc.sync).dma_start(out_rows[:, rows, j0 : j0 + w], result[:])
+                nc.scalar.activation(result[:, t, :], summed[:, t, :], SILU, bias=bias[:, t0 + t : t0 + t + 1])
+            queue.dma_start(out_rows[:, t0 : t0 + count, j0 : j0 + w], result[:])
 
-        finish("a", nc.gpsimd, 0, slice(0, NT), "stage2")
-        finish("b", nc.gpsimd, 1, slice(0, NT), "stage1")
+        for j0, w in SLICES[0:2]:
+            for c in range(PICKS):
+                gather(2, c, j0, j0 + w)
+        both_picks(0)
+        gather(2, 0, HALF, J)
+        gather(3, 1, HALF, J)
+        gather(2, 1, HALF, J)
+        both_picks(1)
+        weigh(0, 0)
+        one_pick(2, 0)
+        weigh(0, 1)
+        one_pick(2, 1)
+        project(2, codes[2], scales[2], HALF)
+        weigh(1, 0)
+        weigh(1, 1)
         for t in range(NT):
-            finish(f"c{t}", nc.gpsimd if t < 1 else nc.vector, 2, slice(t, t + 1), f"last{t}")
+            weigh(2, t)
+
+        finish(nc.gpsimd, nc.sync, 0, 0, NT, stages[3][:].rearrange("p (t j) -> p t j", t=NT))
+        finish(nc.gpsimd, nc.sync, 1, 0, NT, stages[2][:].rearrange("p (t j) -> p t j", t=NT))
+        for t in range(NT):
+            summed = stages[t // 2][:, (t % 2) * HALF : (t % 2 + 1) * HALF].rearrange("p (t j) -> p t j", t=1)
+            finish(nc.gpsimd if t < 1 else nc.vector, nc.sync if t < NT - 1 else nc.scalar, 2, t, 1, summed)

@@ -69,13 +69,14 @@ def tile_list_soft_silu_kernel(tc, xT, wgt, w_words, w_scales, iw0, iw1, b, offs
             nc.sync.dma_start(w_plane[32 * q : 32 * q + 4, :].bitcast(I32), w_scales[0, 4 * q : 4 * q + 4, :].bitcast(I32))
 
         pool_w = [keep.tile([P, PICKS, NT, HALF], F32, name=f"pool_w{h}") for h in range(2)]
-        for h in range(2):
+        for h, t0, t1 in ((0, 0, 4), (1, 0, 2), (1, 2, 4)):
             for c, iw in enumerate((iw0, iw1)):
-                nc.sync.dma_start(pool_w[h][:, c], iw[:, h * HALF : (h + 1) * HALF].rearrange("(t p) j -> p t j", p=P))
+                rows = iw[t0 * P : t1 * P, h * HALF : (h + 1) * HALF]
+                nc.sync.dma_start(pool_w[h][:, c, t0:t1], rows.rearrange("(t p) j -> p t j", p=P))
 
-        bias = keep.tile([P, NT], F32, name="bias")
+        bias = keep.tile([P, NT, 8], F32, name="bias")
         with nc.allow_non_contiguous_dma(reason="one bias value a partition"):
-            nc.sync.dma_start(bias[:], b.rearrange("(t p) -> p t", p=P))
+            nc.sync.dma_start(bias[:, :, 0:1], b.rearrange("(t p o) -> p t o", p=P, o=1))
 
 
         def gather(i, c, j0, j1):
@@ -129,6 +130,8 @@ def tile_list_soft_silu_kernel(tc, xT, wgt, w_words, w_scales, iw0, iw1, b, offs
         terms = [keep.tile([P, PICKS, NT, w], F32, name=f"terms{s}") for s, (j0, w) in enumerate(SLICES)]
         stages = [keep.tile([P, BANK], F32, name=f"stage{n}", align_bytes=64) for n in range(4)]
 
+        wide_banks = [psum.tile([P, 1, PICKS, HALF], F32, name=f"wide{t}") for t in range(NT)]
+
         def both_picks(s):
             j0, w = SLICES[s]
             woven = stages[s][:].bitcast(BF16).rearrange("p (c w i) -> p c w i", c=PICKS, i=PACK)
@@ -138,7 +141,18 @@ def tile_list_soft_silu_kernel(tc, xT, wgt, w_words, w_scales, iw0, iw1, b, offs
         def one_pick(s, c):
             j0, w = SLICES[s]
             woven = stages[s + c][:].bitcast(BF16).rearrange("p (c w i) -> p c w i", c=1, i=PACK)
-            quantise(woven, codes[s][:, c * w : (c + 1) * w], scales[s][:, c * w : (c + 1) * w], j0, w, slice(c, c + 1))
+            cols = slice(c * w, (c + 1) * w)
+            quantise(woven, codes[s][:, cols], scales[s][:, cols], j0, w, slice(c, c + 1))
+            for t in range(NT):
+                nc.tensor.matmul_mx(
+                    wide_banks[t][:, 0, c, :],
+                    lhsT=w_codes[:, 2 * P * t : 2 * P * (t + 1)].bitcast(FP4X4),
+                    lhsT_scale=w_plane[:, P * t : P * (t + 1)],
+                    rhs=codes[s][:, cols].bitcast(FP8X4),
+                    rhs_scale=scales[s][:, cols],
+                    start=True,
+                    stop=True,
+                )
 
         def weigh(s, u):
             j0, w = SLICES[s]
@@ -147,8 +161,8 @@ def tile_list_soft_silu_kernel(tc, xT, wgt, w_words, w_scales, iw0, iw1, b, offs
             rows = slice(per_bank * u, per_bank * (u + 1))
             nc.vector.tensor_tensor(
                 terms[s][:, :, rows, :].rearrange("p c t j -> p t c j"),
-                banks.pop(0)[:],
                 pool_w[h][:, :, rows, jh : jh + w].rearrange("p c t j -> p t c j"),
+                banks.pop(0)[:],
                 MULT,
             )
 
@@ -159,7 +173,7 @@ def tile_list_soft_silu_kernel(tc, xT, wgt, w_words, w_scales, iw0, iw1, b, offs
             result = keep.tile([P, count, w], F32, name=f"result{s}_{t0}")
             engine.tensor_tensor(summed, terms[s][:, 0, t0 : t0 + count, :], terms[s][:, 1, t0 : t0 + count, :], ADD)
             for t in range(count):
-                nc.scalar.activation(result[:, t, :], summed[:, t, :], SILU, bias=bias[:, t0 + t : t0 + t + 1])
+                nc.scalar.activation(result[:, t, :], summed[:, t, :], SILU, bias=bias[:, t0 + t, 0:1])
             queue.dma_start(out_rows[:, t0 : t0 + count, j0 : j0 + w], result[:])
 
         for j0, w in SLICES[0:2]:
@@ -174,7 +188,7 @@ def tile_list_soft_silu_kernel(tc, xT, wgt, w_words, w_scales, iw0, iw1, b, offs
         one_pick(2, 0)
         weigh(0, 1)
         one_pick(2, 1)
-        project(2, codes[2], scales[2], HALF)
+        banks.extend(wide_banks)
         weigh(1, 0)
         weigh(1, 1)
         for t in range(NT):

@@ -20,13 +20,27 @@ SILU = mybir.ActivationFunctionType.Silu
 P = 128
 PACK = 4
 PICKS = 2
+GROUP = 16
+QUAD = 32
 NT = N // P
 BANK = 512
-RUN = 64
-DEAL_STEP = PICKS * J - RUN
-DEAL_START = 7 * PICKS * J + J - RUN
-SLICES = ((0, 128), (128, 128), (256, 256))
 HALF = J // 2
+LINE = 4
+BIAS_PITCH = 8
+
+SLICES = ((0, HALF // 2), (HALF // 2, HALF // 2), (HALF, HALF))
+WIDE = len(SLICES) - 1
+GPSIMD_TILES = 1
+
+WHOLE_PLANES = (0, 1)
+SPLIT_PLANE = 3
+LAST_PLANE = 2
+
+RUN = 64
+RUNS = J // RUN
+DEAL_ROW = 7
+DEAL_STEP = PICKS * J - RUN
+DEAL_START = DEAL_ROW * PICKS * J + J - RUN
 
 
 def tile_list_soft_silu_kernel(tc, xT, wgt, w_words, w_scales, iw0, iw1, b, offs, out):
@@ -37,117 +51,82 @@ def tile_list_soft_silu_kernel(tc, xT, wgt, w_words, w_scales, iw0, iw1, b, offs
 
         x_rows = xT.rearrange("(p i) t -> i p t", i=PACK)
         planes = [keep.tile([P, T], F32, name=f"plane{i}") for i in range(PACK)]
-        work = keep.tile([P, (PACK + 1) * PICKS, J], F32, name="work", align_bytes=64)
+        work = keep.tile([P, PACK * PICKS + 1, J], F32, name="work", align_bytes=64)
         picked = work[:, 0 : PACK * PICKS, :].rearrange("p (i c) j -> p i c j", c=PICKS)
-        head_start = PACK * PICKS * J - HALF
-        head_w = work[:].rearrange("p r j -> p (r j)")[:, head_start : head_start + PICKS * J].rearrange("p (c j) -> p c j", c=PICKS)
-        offsets = keep.tile([P, PICKS * J // 16], U16, name="offsets")
+        first_stage = work[:].rearrange("p r j -> p (r j)")[:, PACK * PICKS * J - HALF : PACK * PICKS * J + HALF]
+        head_w = keep.tile([P, PICKS, J], F32, name="head_w", align_bytes=64)
+        offsets = keep.tile([P, PICKS * J // GROUP], U16, name="offsets")
+
         dealt = keep.tile([P, PICKS, RUN], F32, name="dealt", align_bytes=64)
         flat = wgt.rearrange("r c -> (r c)")[DEAL_START : DEAL_START + P * DEAL_STEP].rearrange("(p s) -> p s", s=DEAL_STEP)
-        nc.sync.dma_start(dealt[:], flat[:, 0 : J + RUN].rearrange("p (c j) -> p c j", j=RUN)[:, 0 : J // RUN + 1 : J // RUN, :])
-        nc.sync.dma_start(planes[0][:], x_rows[0])
+        nc.sync.dma_start(dealt[:], flat[:, 0 : J + RUN].rearrange("p (m j) -> p m j", j=RUN)[:, 0 : RUNS + 1 : RUNS, :])
+        nc.sync.dma_start(planes[WHOLE_PLANES[0]][:], x_rows[WHOLE_PLANES[0]])
         nc.sync.dma_start(offsets[:], offs)
-        for i in (1, 3, 2):
+        for i in (WHOLE_PLANES[1], SPLIT_PLANE, LAST_PLANE):
             nc.sync.dma_start(planes[i][:], x_rows[i])
 
-        turned = keep.tile([P, PICKS, 2, 2, 16], F32, name="turned", align_bytes=64)
+        turned = keep.tile([P, PICKS, RUN // QUAD, QUAD // GROUP, GROUP], F32, name="turned", align_bytes=64)
         nc.vector.transpose(turned[:].rearrange("p c u e a -> p (c u e a)"), dealt[:].rearrange("p c j -> p (c j)"))
         for c in range(PICKS):
-            spread = keep.tile([P, J], F32, name=f"spread{c}", align_bytes=64)
-            nc.vector.tensor_copy(
-                spread[:].rearrange("p (m u e r) -> p m u e r", u=2, e=2, r=16),
-                turned[:, c].rearrange("p u e (a o) -> p a u e o", o=1)[:, 0:8][:, ::-1].to_broadcast([P, 8, 2, 2, 16]),
-            )
-            nc.vector.transpose(head_w[:, c], spread[:])
+            spread = keep.tile([P, RUNS, RUN // QUAD, QUAD // GROUP, GROUP], F32, name=f"spread{c}", align_bytes=64)
+            ascending = turned[:, c].rearrange("p u e (a o) -> p a u e o", o=1)[:, 0:RUNS][:, ::-1]
+            nc.vector.tensor_copy(spread[:], ascending.to_broadcast([P, RUNS, RUN // QUAD, QUAD // GROUP, GROUP]))
+            nc.vector.transpose(head_w[:, c], spread[:].rearrange("p m u e r -> p (m u e r)"))
 
         w_codes = keep.tile([P, 2 * N], U8, name="w_codes", align_bytes=64)
         nc.sync.dma_start(w_codes[:].bitcast(I32), w_words[0].bitcast(I32))
+        w_scale = keep.tile([P, N], U8, name="w_scale", align_bytes=64)
+        nc.gpsimd.memset(w_scale[:].bitcast(I32), 0)
+        for q in range(P // QUAD):
+            nc.sync.dma_start(w_scale[QUAD * q : QUAD * q + 4, :].bitcast(I32), w_scales[0, 4 * q : 4 * q + 4, :].bitcast(I32))
 
-        w_plane = keep.tile([P, N], U8, name="w_plane", align_bytes=64)
-        nc.gpsimd.memset(w_plane[:].bitcast(I32), 0)
-        for q in range(4):
-            nc.sync.dma_start(w_plane[32 * q : 32 * q + 4, :].bitcast(I32), w_scales[0, 4 * q : 4 * q + 4, :].bitcast(I32))
-
-        pool_w = [keep.tile([P, PICKS, NT, HALF], F32, name=f"pool_w{h}") for h in range(2)]
-        for h, t0, t1 in ((0, 0, 4), (1, 0, 2), (1, 2, 4)):
+        pool_w = [keep.tile([P, PICKS, NT, HALF], F32, name=f"pool_w{h}") for h in range(J // HALF)]
+        for h, t0, t1 in ((0, 0, NT), (1, 0, NT // 2), (1, NT // 2, NT)):
             for c, iw in enumerate((iw0, iw1)):
                 rows = iw[t0 * P : t1 * P, h * HALF : (h + 1) * HALF]
                 nc.sync.dma_start(pool_w[h][:, c, t0:t1], rows.rearrange("(t p) j -> p t j", p=P))
 
-        bias = keep.tile([P, NT, 8], F32, name="bias")
-        with nc.allow_non_contiguous_dma(reason="one bias value a partition"):
+        bias = keep.tile([P, NT, BIAS_PITCH], F32, name="bias")
+        with nc.allow_non_contiguous_dma(reason="one bias value a partition and row tile"):
             nc.sync.dma_start(bias[:, :, 0:1], b.rearrange("(t p o) -> p t o", p=P, o=1))
 
-
-        def gather(i, c, j0, j1):
-            first = (c * J + j0) // 16
-            last = (c * J + j1) // 16
-            nc.vector.tensor_tensor(picked[:, i, c, j0:j1], planes[i][:].indirect(offsets[:, first:last]), head_w[:, c, j0:j1], MULT)
-
-        for i in (0, 1):
+        def gather(i, first, last):
             nc.vector.tensor_tensor(
-                picked[:, i].rearrange("p c j -> p (c j)"),
-                planes[i][:].indirect(offsets[:]),
-                head_w.rearrange("p c j -> p (c j)"),
+                picked[:, i].rearrange("p c j -> p (c j)")[:, first:last],
+                planes[i][:].indirect(offsets[:, first // GROUP : last // GROUP]),
+                head_w[:].rearrange("p c j -> p (c j)")[:, first:last],
                 MULT,
             )
-        held = PICKS * J - HALF
-        nc.vector.tensor_tensor(
-            picked[:, 3].rearrange("p c j -> p (c j)")[:, 0:held],
-            planes[3][:].indirect(offsets[:, 0 : held // 16]),
-            head_w.rearrange("p c j -> p (c j)")[:, 0:held],
-            MULT,
-        )
 
-        def quantise(woven, codes, scales, j0, w, picks):
-            nc.scalar.copy(
-                woven.rearrange("p c (g e) i -> p c g i e", e=4),
-                picked[:, :, picks, j0 : j0 + w].rearrange("p i c (g e) -> p c g i e", e=4),
-            )
-            nc.vector.quantize_mx(codes.bitcast(FP8X4), scales, woven.rearrange("p c w i -> p (c w i)"))
-
-        banks = []
-
-        def project(s, codes, scales, w):
-            per_bank = BANK // (PICKS * w)
-            for u in range(NT // per_bank):
-                bank = psum.tile([P, per_bank, PICKS, w], F32, name=f"bank{s}_{u}")
-                banks.append(bank)
-                for v in range(per_bank):
-                    t = per_bank * u + v
-                    nc.tensor.matmul_mx(
-                        bank[:, v].rearrange("p c j -> p (c j)"),
-                        lhsT=w_codes[:, 2 * P * t : 2 * P * (t + 1)].bitcast(FP4X4),
-                        lhsT_scale=w_plane[:, P * t : P * (t + 1)],
-                        rhs=codes[:].bitcast(FP8X4),
-                        rhs_scale=scales[:],
-                        start=True,
-                        stop=True,
-                    )
+        for i in WHOLE_PLANES:
+            gather(i, 0, PICKS * J)
+        gather(SPLIT_PLANE, 0, J + HALF)
 
         codes = [keep.tile([P, PICKS * w], U32, name=f"codes{s}", align_bytes=64) for s, (j0, w) in enumerate(SLICES)]
         scales = [keep.tile([P, PICKS * w], U8, name=f"scales{s}", align_bytes=64) for s, (j0, w) in enumerate(SLICES)]
         terms = [keep.tile([P, PICKS, NT, w], F32, name=f"terms{s}") for s, (j0, w) in enumerate(SLICES)]
-        stages = [keep.tile([P, BANK], F32, name=f"stage{n}", align_bytes=64) for n in range(4)]
+        stages = [first_stage] + [keep.tile([P, BANK], F32, name=f"stage{m}", align_bytes=64)[:] for m in range(1, WIDE + PICKS)]
+        tiles_in_bank = [BANK // (PICKS * w) for j0, w in SLICES]
+        banks = [
+            [psum.tile([P, tiles_in_bank[s], PICKS, w], F32, name=f"bank{s}_{u}") for u in range(NT // tiles_in_bank[s])]
+            for s, (j0, w) in enumerate(SLICES)
+        ]
 
-        wide_banks = [psum.tile([P, 1, PICKS, HALF], F32, name=f"wide{t}") for t in range(NT)]
-
-        def both_picks(s):
+        def project(s, c0, c1):
             j0, w = SLICES[s]
-            woven = stages[s][:].bitcast(BF16).rearrange("p (c w i) -> p c w i", c=PICKS, i=PACK)
-            quantise(woven, codes[s][:], scales[s][:], j0, w, slice(0, PICKS))
-            project(s, codes[s], scales[s], w)
-
-        def one_pick(s, c):
-            j0, w = SLICES[s]
-            woven = stages[s + c][:].bitcast(BF16).rearrange("p (c w i) -> p c w i", c=1, i=PACK)
-            cols = slice(c * w, (c + 1) * w)
-            quantise(woven, codes[s][:, cols], scales[s][:, cols], j0, w, slice(c, c + 1))
+            woven = stages[s + c0].bitcast(BF16).rearrange("p (c w i) -> p c w i", c=c1 - c0, i=PACK)
+            cols = slice(c0 * w, c1 * w)
+            nc.scalar.copy(
+                woven.rearrange("p c (g e) i -> p c g i e", e=LINE),
+                picked[:, :, c0:c1, j0 : j0 + w].rearrange("p i c (g e) -> p c g i e", e=LINE),
+            )
+            nc.vector.quantize_mx(codes[s][:, cols].bitcast(FP8X4), scales[s][:, cols], woven.rearrange("p c w i -> p (c w i)"))
             for t in range(NT):
+                u, v = divmod(t, tiles_in_bank[s])
                 nc.tensor.matmul_mx(
-                    wide_banks[t][:, 0, c, :],
+                    banks[s][u][:, v].rearrange("p c j -> p (c j)")[:, cols],
                     lhsT=w_codes[:, 2 * P * t : 2 * P * (t + 1)].bitcast(FP4X4),
-                    lhsT_scale=w_plane[:, P * t : P * (t + 1)],
+                    lhsT_scale=w_scale[:, P * t : P * (t + 1)],
                     rhs=codes[s][:, cols].bitcast(FP8X4),
                     rhs_scale=scales[s][:, cols],
                     start=True,
@@ -157,12 +136,11 @@ def tile_list_soft_silu_kernel(tc, xT, wgt, w_words, w_scales, iw0, iw1, b, offs
         def weigh(s, u):
             j0, w = SLICES[s]
             h, jh = divmod(j0, HALF)
-            per_bank = BANK // (PICKS * w)
-            rows = slice(per_bank * u, per_bank * (u + 1))
+            tiles = slice(tiles_in_bank[s] * u, tiles_in_bank[s] * (u + 1))
             nc.vector.tensor_tensor(
-                terms[s][:, :, rows, :].rearrange("p c t j -> p t c j"),
-                pool_w[h][:, :, rows, jh : jh + w].rearrange("p c t j -> p t c j"),
-                banks.pop(0)[:],
+                terms[s][:, :, tiles, :].rearrange("p c t j -> p t c j"),
+                pool_w[h][:, :, tiles, jh : jh + w].rearrange("p c t j -> p t c j"),
+                banks[s][u][:],
                 MULT,
             )
 
@@ -176,26 +154,24 @@ def tile_list_soft_silu_kernel(tc, xT, wgt, w_words, w_scales, iw0, iw1, b, offs
                 nc.scalar.activation(result[:, t, :], summed[:, t, :], SILU, bias=bias[:, t0 + t, 0:1])
             queue.dma_start(out_rows[:, t0 : t0 + count, j0 : j0 + w], result[:])
 
-        for j0, w in SLICES[0:2]:
+        for j0, w in SLICES[0:WIDE]:
             for c in range(PICKS):
-                gather(2, c, j0, j0 + w)
-        both_picks(0)
-        gather(2, 0, HALF, J)
-        gather(3, 1, HALF, J)
-        gather(2, 1, HALF, J)
-        both_picks(1)
+                gather(LAST_PLANE, c * J + j0, c * J + j0 + w)
+        project(0, 0, PICKS)
+        for c in range(PICKS):
+            gather(LAST_PLANE, c * J + HALF, (c + 1) * J)
+        gather(SPLIT_PLANE, J + HALF, PICKS * J)
+        project(1, 0, PICKS)
         weigh(0, 0)
-        one_pick(2, 0)
+        project(WIDE, 0, 1)
         weigh(0, 1)
-        one_pick(2, 1)
-        banks.extend(wide_banks)
-        weigh(1, 0)
-        weigh(1, 1)
-        for t in range(NT):
-            weigh(2, t)
+        project(WIDE, 1, 2)
+        for s in range(1, len(SLICES)):
+            for u in range(len(banks[s])):
+                weigh(s, u)
 
-        finish(nc.gpsimd, nc.sync, 0, 0, NT, stages[3][:].rearrange("p (t j) -> p t j", t=NT))
-        finish(nc.gpsimd, nc.sync, 1, 0, NT, stages[2][:].rearrange("p (t j) -> p t j", t=NT))
+        for s in range(WIDE):
+            finish(nc.gpsimd, nc.sync, s, 0, NT, stages[len(stages) - 1 - s].rearrange("p (t j) -> p t j", t=NT))
         for t in range(NT):
-            summed = stages[t // 2][:, (t % 2) * HALF : (t % 2 + 1) * HALF].rearrange("p (t j) -> p t j", t=1)
-            finish(nc.gpsimd if t < 1 else nc.vector, nc.sync if t < NT - 1 else nc.scalar, 2, t, 1, summed)
+            summed = keep.tile([P, 1, HALF], F32, name=f"summed{t}")
+            finish(nc.gpsimd if t < GPSIMD_TILES else nc.vector, nc.sync if t < NT - 1 else nc.scalar, WIDE, t, 1, summed[:])

from contextlib import ExitStack

import concourse.mybir as mybir

K, N, T, J = 512, 512, 2048, 512
FLOPS = 2 * K * N * 2 * J

F32 = mybir.dt.float32
BF16 = mybir.dt.bfloat16
I32 = mybir.dt.int32
U32 = mybir.dt.uint32
U16 = mybir.dt.uint16
U8 = mybir.dt.uint8
FP8X4 = mybir.dt.float8_e4m3fn_x4
FP4X4 = mybir.dt.float4_e2m1fn_x4
MULT = mybir.AluOpType.mult
ADD = mybir.AluOpType.add
SILU = mybir.ActivationFunctionType.Silu

P = 128
PACK = 4
PICKS = 2
GROUP = 16
QUAD = 32
NT = N // P
BANK = 512
HALF = J // 2
LINE = 4
BIAS_PITCH = 8

SLICES = ((0, HALF // 2), (HALF // 2, HALF // 2), (HALF, HALF))
WIDE = len(SLICES) - 1
GPSIMD_TILES = 1

WHOLE_PLANES = (0, 1)
SPLIT_PLANE = 3
LAST_PLANE = 2

RUN = 64
RUNS = J // RUN
DEAL_ROW = 7
DEAL_STEP = PICKS * J - RUN
DEAL_START = DEAL_ROW * PICKS * J + J - RUN


def tile_list_soft_silu_kernel(tc, xT, wgt, w_words, w_scales, iw0, iw1, b, offs, out):
    nc = tc.nc
    with ExitStack() as ctx:
        keep = ctx.enter_context(tc.tile_pool(name="keep", bufs=1))
        psum = ctx.enter_context(tc.psum_pool(name="psum", bufs=1))

        x_rows = xT.rearrange("(p i) t -> i p t", i=PACK)
        planes = [keep.tile([P, T], F32, name=f"plane{i}") for i in range(PACK)]
        work = keep.tile([P, PACK * PICKS + 1, J], F32, name="work", align_bytes=64)
        picked = work[:, 0 : PACK * PICKS, :].rearrange("p (i c) j -> p i c j", c=PICKS)
        first_stage = work[:].rearrange("p r j -> p (r j)")[:, PACK * PICKS * J - HALF : PACK * PICKS * J + HALF]
        head_w = keep.tile([P, PICKS, J], F32, name="head_w", align_bytes=64)
        offsets = keep.tile([P, PICKS * J // GROUP], U16, name="offsets")

        dealt = keep.tile([P, PICKS, RUN], F32, name="dealt", align_bytes=64)
        flat = wgt.rearrange("r c -> (r c)")[DEAL_START : DEAL_START + P * DEAL_STEP].rearrange("(p s) -> p s", s=DEAL_STEP)
        nc.sync.dma_start(dealt[:], flat[:, 0 : J + RUN].rearrange("p (m j) -> p m j", j=RUN)[:, 0 : RUNS + 1 : RUNS, :])
        nc.sync.dma_start(planes[WHOLE_PLANES[0]][:], x_rows[WHOLE_PLANES[0]])
        nc.sync.dma_start(offsets[:], offs)
        for i in (WHOLE_PLANES[1], SPLIT_PLANE, LAST_PLANE):
            nc.sync.dma_start(planes[i][:], x_rows[i])

        turned = keep.tile([P, PICKS, RUN // QUAD, QUAD // GROUP, GROUP], F32, name="turned", align_bytes=64)
        nc.vector.transpose(turned[:].rearrange("p c u e a -> p (c u e a)"), dealt[:].rearrange("p c j -> p (c j)"))
        for c in range(PICKS):
            spread = keep.tile([P, RUNS, RUN // QUAD, QUAD // GROUP, GROUP], F32, name=f"spread{c}", align_bytes=64)
            ascending = turned[:, c].rearrange("p u e (a o) -> p a u e o", o=1)[:, 0:RUNS][:, ::-1]
            nc.vector.tensor_copy(spread[:], ascending.to_broadcast([P, RUNS, RUN // QUAD, QUAD // GROUP, GROUP]))
            nc.vector.transpose(head_w[:, c], spread[:].rearrange("p m u e r -> p (m u e r)"))

        w_codes = keep.tile([P, 2 * N], U8, name="w_codes", align_bytes=64)
        nc.sync.dma_start(w_codes[:].bitcast(I32), w_words[0].bitcast(I32))
        w_scale = keep.tile([P, N], U8, name="w_scale", align_bytes=64)
        nc.gpsimd.memset(w_scale[:].bitcast(I32), 0)
        for q in range(P // QUAD):
            nc.sync.dma_start(w_scale[QUAD * q : QUAD * q + 4, :].bitcast(I32), w_scales[0, 4 * q : 4 * q + 4, :].bitcast(I32))

        pool_w = [keep.tile([P, PICKS, NT, HALF], F32, name=f"pool_w{h}") for h in range(J // HALF)]
        for h, t0, t1 in ((0, 0, NT), (1, 0, NT // 2), (1, NT // 2, NT)):
            for c, iw in enumerate((iw0, iw1)):
                rows = iw[t0 * P : t1 * P, h * HALF : (h + 1) * HALF]
                nc.sync.dma_start(pool_w[h][:, c, t0:t1], rows.rearrange("(t p) j -> p t j", p=P))

        bias = keep.tile([P, NT, BIAS_PITCH], F32, name="bias")
        with nc.allow_non_contiguous_dma(reason="one bias value a partition and row tile"):
            nc.sync.dma_start(bias[:, :, 0:1], b.rearrange("(t p o) -> p t o", p=P, o=1))

        def gather(i, first, last):
            nc.vector.tensor_tensor(
                picked[:, i].rearrange("p c j -> p (c j)")[:, first:last],
                planes[i][:].indirect(offsets[:, first // GROUP : last // GROUP]),
                head_w[:].rearrange("p c j -> p (c j)")[:, first:last],
                MULT,
            )

        for i in WHOLE_PLANES:
            gather(i, 0, PICKS * J)
        gather(SPLIT_PLANE, 0, J + HALF)

        codes = [keep.tile([P, PICKS * w], U32, name=f"codes{s}", align_bytes=64) for s, (j0, w) in enumerate(SLICES)]
        scales = [keep.tile([P, PICKS * w], U8, name=f"scales{s}", align_bytes=64) for s, (j0, w) in enumerate(SLICES)]
        terms = [keep.tile([P, PICKS, NT, w], F32, name=f"terms{s}") for s, (j0, w) in enumerate(SLICES)]
        stages = [first_stage] + [keep.tile([P, BANK], F32, name=f"stage{m}", align_bytes=64)[:] for m in range(1, WIDE + PICKS)]
        tiles_in_bank = [BANK // (PICKS * w) for j0, w in SLICES]
        banks = [
            [psum.tile([P, tiles_in_bank[s], PICKS, w], F32, name=f"bank{s}_{u}") for u in range(NT // tiles_in_bank[s])]
            for s, (j0, w) in enumerate(SLICES)
        ]

        def project(s, c0, c1):
            j0, w = SLICES[s]
            woven = stages[s + c0].bitcast(BF16).rearrange("p (c w i) -> p c w i", c=c1 - c0, i=PACK)
            cols = slice(c0 * w, c1 * w)
            nc.scalar.copy(
                woven.rearrange("p c (g e) i -> p c g i e", e=LINE),
                picked[:, :, c0:c1, j0 : j0 + w].rearrange("p i c (g e) -> p c g i e", e=LINE),
            )
            nc.vector.quantize_mx(codes[s][:, cols].bitcast(FP8X4), scales[s][:, cols], woven.rearrange("p c w i -> p (c w i)"))
            for t in range(NT):
                u, v = divmod(t, tiles_in_bank[s])
                nc.tensor.matmul_mx(
                    banks[s][u][:, v].rearrange("p c j -> p (c j)")[:, cols],
                    lhsT=w_codes[:, 2 * P * t : 2 * P * (t + 1)].bitcast(FP4X4),
                    lhsT_scale=w_scale[:, P * t : P * (t + 1)],
                    rhs=codes[s][:, cols].bitcast(FP8X4),
                    rhs_scale=scales[s][:, cols],
                    start=True,
                    stop=True,
                )

        def weigh(s, u):
            j0, w = SLICES[s]
            h, jh = divmod(j0, HALF)
            tiles = slice(tiles_in_bank[s] * u, tiles_in_bank[s] * (u + 1))
            nc.vector.tensor_tensor(
                terms[s][:, :, tiles, :].rearrange("p c t j -> p t c j"),
                pool_w[h][:, :, tiles, jh : jh + w].rearrange("p c t j -> p t c j"),
                banks[s][u][:],
                MULT,
            )

        out_rows = out.rearrange("(t p) j -> p t j", p=P)

        def finish(engine, queue, s, t0, count, summed):
            j0, w = SLICES[s]
            result = keep.tile([P, count, w], F32, name=f"result{s}_{t0}")
            engine.tensor_tensor(summed, terms[s][:, 0, t0 : t0 + count, :], terms[s][:, 1, t0 : t0 + count, :], ADD)
            for t in range(count):
                nc.scalar.activation(result[:, t, :], summed[:, t, :], SILU, bias=bias[:, t0 + t, 0:1])
            queue.dma_start(out_rows[:, t0 : t0 + count, j0 : j0 + w], result[:])

        for j0, w in SLICES[0:WIDE]:
            for c in range(PICKS):
                gather(LAST_PLANE, c * J + j0, c * J + j0 + w)
        project(0, 0, PICKS)
        for c in range(PICKS):
            gather(LAST_PLANE, c * J + HALF, (c + 1) * J)
        gather(SPLIT_PLANE, J + HALF, PICKS * J)
        project(1, 0, PICKS)
        weigh(0, 0)
        project(WIDE, 0, 1)
        weigh(0, 1)
        project(WIDE, 1, 2)
        for s in range(1, len(SLICES)):
            for u in range(len(banks[s])):
                weigh(s, u)

        for s in range(WIDE):
            finish(nc.gpsimd, nc.sync, s, 0, NT, stages[len(stages) - 1 - s].rearrange("p (t j) -> p t j", t=NT))
        for t in range(NT):
            summed = keep.tile([P, 1, HALF], F32, name=f"summed{t}")
            finish(nc.gpsimd if t < GPSIMD_TILES else nc.vector, nc.sync if t < NT - 1 else nc.scalar, WIDE, t, 1, summed[:])
